import numpy as np
import ml_dtypes


def mxq(x, axis, fmt="e4m3"):
    dtype, down = {"e4m3": (ml_dtypes.float8_e4m3fn, 7), "e5m2": (ml_dtypes.float8_e5m2, 14)}[fmt]
    v = np.moveaxis(np.asarray(x, np.float32).astype(ml_dtypes.bfloat16).astype(np.float64), axis, -1)
    blocks = v.reshape(v.shape[:-1] + (-1, 32))
    amax = np.abs(blocks).max(-1, keepdims=True)
    byte = np.maximum(np.where(amax > 0, np.frexp(amax)[1] - 1 + 127, 0) - down, 1)
    scale = np.exp2(byte - 127.0)
    codes = (blocks / scale).astype(np.float32).astype(dtype).astype(np.float64)
    return np.moveaxis((codes * scale).reshape(v.shape), -1, axis)


WIDE = False


def mx_kscale(k, group=512):
    if not WIDE:
        return np.ones(k)
    levels = np.array([18, -18])
    if group != 512:
        return np.exp2(np.random.permutation(np.resize(levels, k // group))).repeat(group)
    if k % 512:
        return np.exp2(np.random.permutation(np.resize(levels, k // 32))).repeat(32)
    a = np.empty((k // 512, 16))
    for p in range(k // 512):
        a[p, :8] = np.random.permutation(np.resize(levels, 8))
        for g in range(8):
            far = levels[np.abs(levels - a[p, g]) >= 10]
            a[p, g + 8] = far[np.random.randint(len(far))]
    return np.exp2(a.ravel()).repeat(32)


def f64(x):
    return np.asarray(x).astype(np.float64)


G, D, I, F, E = 8, 128, 128, 128, 128


def sgn(shape):
    return np.random.uniform(0.5, 2.0, shape) * np.where(np.random.standard_normal(shape) < 0, -1.0, 1.0)


def setup_inputs():
    n = np.random.standard_normal
    s_d = mx_kscale(D, 0)
    s_i = mx_kscale(I, 0)
    return {
        "kT": (n((G, D, I)) / np.sqrt(D) / s_d[:, None]).astype(np.float32),
        "S": (n((G, D, E)) * s_d[:, None]).astype(np.float32),
        "v": (n((G, I, E))).astype(np.float32),
        "be": (sgn((G, I, 1)) * s_i[:, None]).astype(np.float32),
        "kn": (n((G, I, F)) / np.sqrt(I) / s_i[:, None] * s_d).astype(np.float32),
    }


def reference(kT, S, v, be, kn):
    kTq = mxq(f64(kT), 1, "e4m3")
    Sq = mxq(f64(S), 1, "e4m3")
    z = kTq.transpose(0, 2, 1) @ Sq
    u = np.tanh(f64(v) - z) * f64(be)
    knq = mxq(f64(kn), 1, "e4m3")
    uq = mxq(u, 1, "e4m3")
    w = knq.transpose(0, 2, 1) @ uq
    o = f64(S) + w
    return o

@@ -1,0 +1,160 @@
+from contextlib import ExitStack
+
+import concourse.mybir as mybir
+
+F32 = mybir.dt.float32
+BF16 = mybir.dt.bfloat16
+U32 = mybir.dt.uint32
+U8 = mybir.dt.uint8
+FP8X4 = mybir.dt.float8_e4m3fn_x4
+ALU = mybir.AluOpType
+ACT = mybir.ActivationFunctionType
+
+G, W = 8, 128
+P = 128
+R = 32
+PACK = 4
+SIDE = 4
+SETS = G // SIDE
+RUN = 4
+
+FLOPS = 2 * 2 * G * W * W * W
+
+
+def tile_rows_upd_huber_kernel(tc, kT, S, v, be, kn, out):
+    nc = tc.nc
+
+    with ExitStack() as ctx:
+        sb = ctx.enter_context(tc.tile_pool(name="sb", bufs=1))
+        ps = ctx.enter_context(tc.psum_pool(name="ps", bufs=1))
+        ctx.enter_context(tc.manual_schedule())
+
+        def tiles(name, shape, dtype, count=SETS):
+            return [sb.tile(shape, dtype, name="%s%d" % (name, n), align_bytes=64) for n in range(count)]
+
+        def packed_rows(x, s):
+            return x[SIDE * s : SIDE * (s + 1)].rearrange("c (p j) w -> (c p) j w", j=PACK)
+
+        def plain_rows(x, g0, g1):
+            return x[g0:g1].rearrange("c r w -> r c w")
+
+        raw = {n: tiles(n + "_raw", [P, PACK, W], F32) for n in ("S", "kT", "kn")}
+        u_moved = tiles("u_moved", [P, PACK, W], BF16)
+        inter = {n: tiles(n + "_int", [P, W, PACK], BF16) for n in ("S", "kT", "kn", "u")}
+        codes = {n: tiles(n + "_codes", [P, W], U32) for n in ("S", "kT", "kn", "u")}
+        scales = {n: tiles(n + "_scales", [P, W], U8) for n in ("S", "kT", "kn", "u")}
+        v_rows = tiles("v_rows", [P, SIDE, W], F32)
+        s_rows = tiles("s_rows", [P, SIDE, W], F32)
+        err = tiles("err", [P, W], F32, G)
+        squashed = tiles("squashed", [P, W], F32, G)
+        u_rows = tiles("u_rows", [P, W], BF16, G)
+        res = tiles("res", [P, 2, W], F32, G // 2)
+        be_raw = sb.tile([P, G * R], F32, name="be_raw", align_bytes=64)
+        be_col = sb.tile([P, G * R], F32, name="be_col", align_bytes=64)
+        warm = sb.tile([P, 1], F32, name="warm")
+        banks = [ps.tile([P, 2, W], F32, name="bank%d" % g) for g in range(G)]
+
+        def interleave(eng, name, s, src):
+            dst = inter[name][s][:].rearrange("p (a i) j -> p a j i", i=RUN)
+            src = src[:].rearrange("p j (a i) -> p a j i", i=RUN)
+            if eng == "vector":
+                nc.vector.tensor_copy(out=dst, in_=src)
+            else:
+                nc.scalar.copy(out=dst, in_=src)
+
+        def quantise(name, s):
+            nc.vector.quantize_mx(
+                out=codes[name][s][:].bitcast(FP8X4),
+                scales=scales[name][s][:],
+                in_=inter[name][s][:].rearrange("p w j -> p (w j)"),
+            )
+
+        def product(s, place, lhs, rhs):
+            for c in range(SIDE):
+                rows = slice(R * c, R * (c + 1))
+                nc.tensor.matmul_mx(
+                    out=banks[SIDE * s + c][:, place, :],
+                    lhsT=codes[lhs][s][rows, :].bitcast(FP8X4),
+                    lhsT_scale=scales[lhs][s][rows, :],
+                    rhs=codes[rhs][s][rows, :].bitcast(FP8X4),
+                    rhs_scale=scales[rhs][s][rows, :],
+                    start=True,
+                    stop=True,
+                )
+
+        def heads(s):
+            return range(SIDE * s, SIDE * (s + 1))
+
+        def errors(s):
+            for g in heads(s):
+                nc.vector.tensor_tensor(out=err[g][:], in0=v_rows[s][:, g % SIDE, :], in1=banks[g][:, 0, :], op=ALU.subtract)
+                nc.scalar.activation(out=squashed[g][:], in_=err[g][:], func=ACT.Tanh)
+
+        def scale(s):
+            for g in heads(s):
+                nc.vector.tensor_scalar(out=u_rows[g][:], in0=squashed[g][:], scalar1=be_col[:, R * g : R * g + 1], scalar2=None, op0=ALU.mult)
+
+        def move(s, queue):
+            for g in heads(s):
+                c = g % SIDE
+                queue.dma_start(out=u_moved[s][R * c : R * (c + 1), :, :], in_=u_rows[g][:])
+
+        def finish(s):
+            for g in heads(s):
+                nc.vector.tensor_tensor(out=res[g // 2][:, g % 2, :], in0=s_rows[s][:, g % SIDE, :], in1=banks[g][:, 1, :], op=ALU.add)
+                if g % 2 == 1:
+                    nc.sync.dma_start(out=plain_rows(out, g - 1, g + 1), in_=res[g // 2][:])
+
+        def load_packed(name, x, s):
+            nc.sync.dma_start(out=raw[name][s][:], in_=packed_rows(x, s))
+
+        def load_plain(dst, x, s):
+            nc.sync.dma_start(out=dst[s][:], in_=plain_rows(x, SIDE * s, SIDE * (s + 1)))
+
+        nc.gpsimd.memset(be_raw[:], 0.0)
+        nc.vector.memset(warm[:], 0.0)
+        nc.scalar.activation(out=warm[:], in_=warm[:], func=ACT.Tanh)
+        load_packed("S", S, 0)
+        load_packed("kT", kT, 0)
+        nc.sync.dma_start(
+            out=be_raw[0:P:R, :].rearrange("q (g a) -> q g a", a=R),
+            in_=be.rearrange("g (q a) o -> q g (a o)", a=R),
+        )
+        load_packed("S", S, 1)
+        load_packed("kT", kT, 1)
+        load_plain(v_rows, v, 0)
+        load_plain(v_rows, v, 1)
+        load_packed("kn", kn, 0)
+
+        interleave("vector", "S", 0, raw["S"][0])
+        quantise("S", 0)
+        interleave("vector", "kT", 0, raw["kT"][0])
+        quantise("kT", 0)
+        product(0, 0, "kT", "S")
+        interleave("vector", "S", 1, raw["S"][1])
+        nc.vector.transpose(out=be_col[:], in_=be_raw[:])
+        interleave("vector", "kT", 1, raw["kT"][1])
+        quantise("S", 1)
+        quantise("kT", 1)
+        product(1, 0, "kT", "S")
+        errors(0)
+        scale(0)
+        move(0, nc.sync)
+        load_packed("kn", kn, 1)
+        load_plain(s_rows, S, 0)
+        load_plain(s_rows, S, 1)
+        errors(1)
+        scale(1)
+        move(1, nc.scalar)
+        interleave("vector", "kn", 0, raw["kn"][0])
+        interleave("scalar", "kn", 1, raw["kn"][1])
+        interleave("vector", "u", 0, u_moved[0])
+        quantise("kn", 0)
+        quantise("u", 0)
+        product(0, 1, "kn", "u")
+        quantise("kn", 1)
+        interleave("vector", "u", 1, u_moved[1])
+        quantise("u", 1)
+        product(1, 1, "kn", "u")
+        finish(0)
+        finish(1)

@@ -38,25 +38,26 @@ def tile_rows_upd_huber_kernel(tc, kT, S, v, be, kn, out):
         def plain_rows(x, g0, g1):
             return x[g0:g1].rearrange("c r w -> r c w")
 
-        raw = {n: tiles(n + "_raw", [P, PACK, W], F32) for n in ("S", "kT", "kn")}
+        raw = {n: tiles(n + "_raw", [P, PACK, W], F32) for n in ("S", "kT")}
+        kn_raw = sb.tile([P, SETS, PACK * W], F32, name="kn_raw")
+        v_last = tiles("v_last", [P, 2, W], F32)
         u_moved = tiles("u_moved", [P, PACK, W], BF16)
         inter = {n: tiles(n + "_int", [P, W, PACK], BF16) for n in ("S", "kT", "kn", "u")}
         codes = {n: tiles(n + "_codes", [P, W], U32) for n in ("S", "kT", "kn", "u")}
         scales = {n: tiles(n + "_scales", [P, W], U8) for n in ("S", "kT", "kn", "u")}
-        v_rows = tiles("v_rows", [P, SIDE, W], F32)
+        v_rows = tiles("v_rows", [P, SIDE, W], F32, 1)
         s_rows = tiles("s_rows", [P, SIDE, W], F32)
         err = tiles("err", [P, W], F32, G)
         squashed = tiles("squashed", [P, W], F32, G)
         u_rows = tiles("u_rows", [P, W], BF16, G)
-        res = tiles("res", [P, 2, W], F32, G // 2)
+        res = tiles("res", [P, W], F32, G)
         be_raw = sb.tile([P, G * R], F32, name="be_raw", align_bytes=64)
         be_col = sb.tile([P, G * R], F32, name="be_col", align_bytes=64)
-        warm = sb.tile([P, 1], F32, name="warm")
         banks = [ps.tile([P, 2, W], F32, name="bank%d" % g) for g in range(G)]
 
         def interleave(eng, name, s, src):
             dst = inter[name][s][:].rearrange("p (a i) j -> p a j i", i=RUN)
-            src = src[:].rearrange("p j (a i) -> p a j i", i=RUN)
+            src = src.rearrange("p j (a i) -> p a j i", i=RUN)
             if eng == "vector":
                 nc.vector.tensor_copy(out=dst, in_=src)
             else:
@@ -85,25 +86,22 @@ def tile_rows_upd_huber_kernel(tc, kT, S, v, be, kn, out):
         def heads(s):
             return range(SIDE * s, SIDE * (s + 1))
 
-        def errors(s):
-            for g in heads(s):
-                nc.vector.tensor_tensor(out=err[g][:], in0=v_rows[s][:, g % SIDE, :], in1=banks[g][:, 0, :], op=ALU.subtract)
-                nc.scalar.activation(out=squashed[g][:], in_=err[g][:], func=ACT.Tanh)
+        def error(g):
+            values = v_rows[0][:, g, :] if g < SIDE else v_last[(g - SIDE) // 2][:, g % 2, :]
+            nc.vector.tensor_tensor(out=err[g][:], in0=values, in1=banks[g][:, 0, :], op=ALU.subtract)
+            nc.scalar.activation(out=squashed[g][:], in_=err[g][:], func=ACT.Tanh)
 
-        def scale(s):
-            for g in heads(s):
-                nc.vector.tensor_scalar(out=u_rows[g][:], in0=squashed[g][:], scalar1=be_col[:, R * g : R * g + 1], scalar2=None, op0=ALU.mult)
+        def scale(g):
+            nc.vector.tensor_scalar(out=u_rows[g][:], in0=squashed[g][:], scalar1=be_col[:, R * g : R * g + 1], scalar2=None, op0=ALU.mult)
 
-        def move(s, queue):
-            for g in heads(s):
-                c = g % SIDE
-                queue.dma_start(out=u_moved[s][R * c : R * (c + 1), :, :], in_=u_rows[g][:])
+        def move(g, queue):
+            s, c = divmod(g, SIDE)
+            queue.dma_start(out=u_moved[s][R * c : R * (c + 1), :, :], in_=u_rows[g][:])
 
-        def finish(s):
-            for g in heads(s):
-                nc.vector.tensor_tensor(out=res[g // 2][:, g % 2, :], in0=s_rows[s][:, g % SIDE, :], in1=banks[g][:, 1, :], op=ALU.add)
-                if g % 2 == 1:
-                    nc.sync.dma_start(out=plain_rows(out, g - 1, g + 1), in_=res[g // 2][:])
+        def finish(g, queue):
+            s, c = divmod(g, SIDE)
+            nc.vector.tensor_tensor(out=res[g][:], in0=s_rows[s][:, c, :], in1=banks[g][:, 1, :], op=ALU.add)
+            queue.dma_start(out=out[g], in_=res[g][:])
 
         def load_packed(name, x, s):
             nc.sync.dma_start(out=raw[name][s][:], in_=packed_rows(x, s))
@@ -112,8 +110,6 @@ def tile_rows_upd_huber_kernel(tc, kT, S, v, be, kn, out):
             nc.sync.dma_start(out=dst[s][:], in_=plain_rows(x, SIDE * s, SIDE * (s + 1)))
 
         nc.gpsimd.memset(be_raw[:], 0.0)
-        nc.vector.memset(warm[:], 0.0)
-        nc.scalar.activation(out=warm[:], in_=warm[:], func=ACT.Tanh)
         load_packed("S", S, 0)
         load_packed("kT", kT, 0)
         nc.sync.dma_start(
@@ -123,38 +119,49 @@ def tile_rows_upd_huber_kernel(tc, kT, S, v, be, kn, out):
         load_packed("S", S, 1)
         load_packed("kT", kT, 1)
         load_plain(v_rows, v, 0)
-        load_plain(v_rows, v, 1)
-        load_packed("kn", kn, 0)
+        for h in range(2):
+            nc.sync.dma_start(out=v_last[h][:], in_=plain_rows(v, SIDE + 2 * h, SIDE + 2 * h + 2))
+        nc.sync.dma_start(out=kn_raw[:], in_=kn.rearrange("(s c) (p j) w -> (c p) s (j w)", c=SIDE, j=PACK))
 
-        interleave("vector", "S", 0, raw["S"][0])
+        interleave("vector", "S", 0, raw["S"][0][:])
         quantise("S", 0)
-        interleave("vector", "kT", 0, raw["kT"][0])
+        interleave("vector", "kT", 0, raw["kT"][0][:])
+        nc.vector.transpose(out=be_col[:], in_=be_raw[:])
         quantise("kT", 0)
         product(0, 0, "kT", "S")
-        interleave("vector", "S", 1, raw["S"][1])
-        nc.vector.transpose(out=be_col[:], in_=be_raw[:])
-        interleave("vector", "kT", 1, raw["kT"][1])
+        interleave("vector", "S", 1, raw["S"][1][:])
+        interleave("vector", "kT", 1, raw["kT"][1][:])
         quantise("S", 1)
         quantise("kT", 1)
         product(1, 0, "kT", "S")
-        errors(0)
+        for g in range(3):
+            error(g)
         scale(0)
-        move(0, nc.sync)
-        load_packed("kn", kn, 1)
+        move(0, nc.scalar)
+        error(3)
+        for g in (1, 2):
+            scale(g)
+            move(g, nc.scalar)
+        error(4)
+        scale(3)
+        move(3, nc.sync)
         load_plain(s_rows, S, 0)
-        load_plain(s_rows, S, 1)
-        errors(1)
-        scale(1)
-        move(1, nc.scalar)
-        interleave("vector", "kn", 0, raw["kn"][0])
-        interleave("scalar", "kn", 1, raw["kn"][1])
-        interleave("vector", "u", 0, u_moved[0])
+        for g in range(5, G):
+            error(g)
+        for g in heads(1):
+            scale(g)
+            move(g, nc.scalar)
+        nc.scalar.dma_start(out=s_rows[1][:], in_=plain_rows(S, SIDE, G))
+        interleave("scalar", "kn", 1, kn_raw[:, 1, :].rearrange("p (j w) -> p j w", j=PACK))
+        interleave("vector", "kn", 0, kn_raw[:, 0, :].rearrange("p (j w) -> p j w", j=PACK))
+        interleave("vector", "u", 0, u_moved[0][:])
         quantise("kn", 0)
         quantise("u", 0)
         product(0, 1, "kn", "u")
         quantise("kn", 1)
-        interleave("vector", "u", 1, u_moved[1])
+        interleave("vector", "u", 1, u_moved[1][:])
+        finish(0, nc.sync)
         quantise("u", 1)
         product(1, 1, "kn", "u")
-        finish(0)
-        finish(1)
+        for g in range(1, G):
+            finish(g, nc.scalar if g % 2 else nc.sync)

@@ -10,15 +10,18 @@ FP8X4 = mybir.dt.float8_e4m3fn_x4
 ALU = mybir.AluOpType
 ACT = mybir.ActivationFunctionType
 
-G, W = 8, 128
+HEADS = 8
+W = 128
 P = 128
-R = 32
+ROWS = 32
 PACK = 4
-SIDE = 4
-SETS = G // SIDE
+SIDE = P // ROWS
+SETS = HEADS // SIDE
+PAIR = 2
 RUN = 4
+LAG = 3
 
-FLOPS = 2 * 2 * G * W * W * W
+FLOPS = 2 * 2 * HEADS * W * W * W
 
 
 def tile_rows_upd_huber_kernel(tc, kT, S, v, be, kn, out):
@@ -29,139 +32,116 @@ def tile_rows_upd_huber_kernel(tc, kT, S, v, be, kn, out):
         ps = ctx.enter_context(tc.psum_pool(name="ps", bufs=1))
         ctx.enter_context(tc.manual_schedule())
 
-        def tiles(name, shape, dtype, count=SETS):
+        def tiles(name, shape, dtype, count):
             return [sb.tile(shape, dtype, name="%s%d" % (name, n), align_bytes=64) for n in range(count)]
 
-        def packed_rows(x, s):
-            return x[SIDE * s : SIDE * (s + 1)].rearrange("c (p j) w -> (c p) j w", j=PACK)
-
-        def plain_rows(x, g0, g1):
-            return x[g0:g1].rearrange("c r w -> r c w")
-
-        raw = {n: tiles(n + "_raw", [P, PACK, W], F32) for n in ("S", "kT")}
+        operands = ("S", "kT", "kn", "u")
+        s_raw = tiles("S_raw", [P, PACK, W], F32, SETS)
+        kt_raw = tiles("kT_raw", [P, PACK, W], F32, SETS)
         kn_raw = sb.tile([P, SETS, PACK * W], F32, name="kn_raw")
-        v_last = tiles("v_last", [P, 2, W], F32)
-        u_moved = tiles("u_moved", [P, PACK, W], BF16)
-        inter = {n: tiles(n + "_int", [P, W, PACK], BF16) for n in ("S", "kT", "kn", "u")}
-        codes = {n: tiles(n + "_codes", [P, W], U32) for n in ("S", "kT", "kn", "u")}
-        scales = {n: tiles(n + "_scales", [P, W], U8) for n in ("S", "kT", "kn", "u")}
-        v_rows = tiles("v_rows", [P, SIDE, W], F32, 1)
-        s_rows = tiles("s_rows", [P, SIDE, W], F32)
-        err = tiles("err", [P, W], F32, G)
-        squashed = tiles("squashed", [P, W], F32, G)
-        u_rows = tiles("u_rows", [P, W], BF16, G)
-        res = tiles("res", [P, W], F32, G)
-        be_raw = sb.tile([P, G * R], F32, name="be_raw", align_bytes=64)
-        be_col = sb.tile([P, G * R], F32, name="be_col", align_bytes=64)
-        banks = [ps.tile([P, 2, W], F32, name="bank%d" % g) for g in range(G)]
+        u_moved = tiles("u_moved", [P, PACK, W], BF16, SETS)
+        grouped = {name: tiles(name + "_grouped", [P, W, PACK], BF16, SETS) for name in operands}
+        codes = {name: tiles(name + "_codes", [P, W], U32, SETS) for name in operands}
+        scales = {name: tiles(name + "_scales", [P, W], U8, SETS) for name in operands}
+        v_rows = tiles("v_rows", [P, PAIR, W], F32, HEADS // PAIR)
+        s_rows = tiles("s_rows", [P, PAIR, W], F32, HEADS // PAIR)
+        err = tiles("err", [P, W], F32, HEADS)
+        squashed = tiles("squashed", [P, W], F32, HEADS)
+        u_rows = tiles("u_rows", [P, W], BF16, HEADS)
+        res = tiles("res", [P, W], F32, HEADS)
+        be_raw = sb.tile([P, HEADS * ROWS], F32, name="be_raw", align_bytes=64)
+        be_col = sb.tile([P, HEADS * ROWS], F32, name="be_col", align_bytes=64)
+        banks = [ps.tile([P, 2, W], F32, name="bank%d" % g) for g in range(HEADS)]
+        z = [bank[:, 0, :] for bank in banks]
+        w = [bank[:, 1, :] for bank in banks]
 
-        def interleave(eng, name, s, src):
-            dst = inter[name][s][:].rearrange("p (a i) j -> p a j i", i=RUN)
-            src = src.rearrange("p j (a i) -> p a j i", i=RUN)
-            if eng == "vector":
-                nc.vector.tensor_copy(out=dst, in_=src)
-            else:
-                nc.scalar.copy(out=dst, in_=src)
+        def load_packed(dst, x, s):
+            rows = x[SIDE * s : SIDE * (s + 1)].rearrange("c (p j) n -> (c p) j n", j=PACK)
+            nc.sync.dma_start(out=dst[s][:], in_=rows)
+
+        def load_plain(dst, x):
+            for n in range(HEADS // PAIR):
+                nc.sync.dma_start(out=dst[n][:], in_=x[PAIR * n : PAIR * (n + 1)].rearrange("c r n -> r c n"))
+
+        def interleave(name, s, rows):
+            nc.vector.tensor_copy(
+                out=grouped[name][s][:].rearrange("p (a i) j -> p a j i", i=RUN),
+                in_=rows.rearrange("p j (a i) -> p a j i", i=RUN),
+            )
 
         def quantise(name, s):
             nc.vector.quantize_mx(
                 out=codes[name][s][:].bitcast(FP8X4),
                 scales=scales[name][s][:],
-                in_=inter[name][s][:].rearrange("p w j -> p (w j)"),
+                in_=grouped[name][s][:].rearrange("p n j -> p (n j)"),
             )
 
-        def product(s, place, lhs, rhs):
+        def product(s, results, stationary, moving):
             for c in range(SIDE):
-                rows = slice(R * c, R * (c + 1))
+                rows = slice(ROWS * c, ROWS * (c + 1))
                 nc.tensor.matmul_mx(
-                    out=banks[SIDE * s + c][:, place, :],
-                    lhsT=codes[lhs][s][rows, :].bitcast(FP8X4),
-                    lhsT_scale=scales[lhs][s][rows, :],
-                    rhs=codes[rhs][s][rows, :].bitcast(FP8X4),
-                    rhs_scale=scales[rhs][s][rows, :],
+                    out=results[SIDE * s + c],
+                    lhsT=codes[stationary][s][rows, :].bitcast(FP8X4),
+                    lhsT_scale=scales[stationary][s][rows, :],
+                    rhs=codes[moving][s][rows, :].bitcast(FP8X4),
+                    rhs_scale=scales[moving][s][rows, :],
                     start=True,
                     stop=True,
                 )
 
-        def heads(s):
-            return range(SIDE * s, SIDE * (s + 1))
-
-        def error(g):
-            values = v_rows[0][:, g, :] if g < SIDE else v_last[(g - SIDE) // 2][:, g % 2, :]
-            nc.vector.tensor_tensor(out=err[g][:], in0=values, in1=banks[g][:, 0, :], op=ALU.subtract)
+        def squash_error(g):
+            nc.vector.tensor_tensor(out=err[g][:], in0=v_rows[g // PAIR][:, g % PAIR, :], in1=z[g], op=ALU.subtract)
             nc.scalar.activation(out=squashed[g][:], in_=err[g][:], func=ACT.Tanh)
 
-        def scale(g):
-            nc.vector.tensor_scalar(out=u_rows[g][:], in0=squashed[g][:], scalar1=be_col[:, R * g : R * g + 1], scalar2=None, op0=ALU.mult)
-
-        def move(g, queue):
+        def scale_and_move(g):
             s, c = divmod(g, SIDE)
-            queue.dma_start(out=u_moved[s][R * c : R * (c + 1), :, :], in_=u_rows[g][:])
+            step = be_col[:, ROWS * g : ROWS * g + 1]
+            nc.vector.tensor_scalar(out=u_rows[g][:], in0=squashed[g][:], scalar1=step, scalar2=None, op0=ALU.mult)
+            nc.sync.dma_start(out=u_moved[s][ROWS * c : ROWS * (c + 1), :, :], in_=u_rows[g][:])
 
-        def finish(g, queue):
-            s, c = divmod(g, SIDE)
-            nc.vector.tensor_tensor(out=res[g][:], in0=s_rows[s][:, c, :], in1=banks[g][:, 1, :], op=ALU.add)
-            queue.dma_start(out=out[g], in_=res[g][:])
-
-        def load_packed(name, x, s):
-            nc.sync.dma_start(out=raw[name][s][:], in_=packed_rows(x, s))
-
-        def load_plain(dst, x, s):
-            nc.sync.dma_start(out=dst[s][:], in_=plain_rows(x, SIDE * s, SIDE * (s + 1)))
+        def add_and_store(g):
+            nc.vector.tensor_tensor(out=res[g][:], in0=s_rows[g // PAIR][:, g % PAIR, :], in1=w[g], op=ALU.add)
+            nc.sync.dma_start(out=out[g], in_=res[g][:])
 
         nc.gpsimd.memset(be_raw[:], 0.0)
-        load_packed("S", S, 0)
-        load_packed("kT", kT, 0)
+        load_packed(s_raw, S, 0)
+        load_packed(kt_raw, kT, 0)
         nc.sync.dma_start(
-            out=be_raw[0:P:R, :].rearrange("q (g a) -> q g a", a=R),
-            in_=be.rearrange("g (q a) o -> q g (a o)", a=R),
+            out=be_raw[0:P:ROWS, :].rearrange("q (g a) -> q g a", a=ROWS),
+            in_=be.rearrange("g (q a) o -> q g (a o)", a=ROWS),
         )
-        load_packed("S", S, 1)
-        load_packed("kT", kT, 1)
-        load_plain(v_rows, v, 0)
-        for h in range(2):
-            nc.sync.dma_start(out=v_last[h][:], in_=plain_rows(v, SIDE + 2 * h, SIDE + 2 * h + 2))
-        nc.sync.dma_start(out=kn_raw[:], in_=kn.rearrange("(s c) (p j) w -> (c p) s (j w)", c=SIDE, j=PACK))
+        load_packed(s_raw, S, 1)
+        load_packed(kt_raw, kT, 1)
+        load_plain(v_rows, v)
+        nc.sync.dma_start(out=kn_raw[:], in_=kn.rearrange("(s c) (p j) n -> (c p) s (j n)", c=SIDE, j=PACK))
 
-        interleave("vector", "S", 0, raw["S"][0][:])
+        interleave("S", 0, s_raw[0][:])
         quantise("S", 0)
-        interleave("vector", "kT", 0, raw["kT"][0][:])
+        interleave("kT", 0, kt_raw[0][:])
         nc.vector.transpose(out=be_col[:], in_=be_raw[:])
         quantise("kT", 0)
-        product(0, 0, "kT", "S")
-        interleave("vector", "S", 1, raw["S"][1][:])
-        interleave("vector", "kT", 1, raw["kT"][1][:])
+        product(0, z, "kT", "S")
+        interleave("S", 1, s_raw[1][:])
+        interleave("kT", 1, kt_raw[1][:])
         quantise("S", 1)
         quantise("kT", 1)
-        product(1, 0, "kT", "S")
-        for g in range(3):
-            error(g)
-        scale(0)
-        move(0, nc.scalar)
-        error(3)
-        for g in (1, 2):
-            scale(g)
-            move(g, nc.scalar)
-        error(4)
-        scale(3)
-        move(3, nc.sync)
-        load_plain(s_rows, S, 0)
-        for g in range(5, G):
-            error(g)
-        for g in heads(1):
-            scale(g)
-            move(g, nc.scalar)
-        nc.scalar.dma_start(out=s_rows[1][:], in_=plain_rows(S, SIDE, G))
-        interleave("scalar", "kn", 1, kn_raw[:, 1, :].rearrange("p (j w) -> p j w", j=PACK))
-        interleave("vector", "kn", 0, kn_raw[:, 0, :].rearrange("p (j w) -> p j w", j=PACK))
-        interleave("vector", "u", 0, u_moved[0][:])
-        quantise("kn", 0)
-        quantise("u", 0)
-        product(0, 1, "kn", "u")
-        quantise("kn", 1)
-        interleave("vector", "u", 1, u_moved[1][:])
-        finish(0, nc.sync)
-        quantise("u", 1)
-        product(1, 1, "kn", "u")
-        for g in range(1, G):
-            finish(g, nc.scalar if g % 2 else nc.sync)
+        product(1, z, "kT", "S")
+
+        for g in range(HEADS + LAG):
+            if g < HEADS:
+                squash_error(g)
+            if g >= LAG:
+                scale_and_move(g - LAG)
+
+        load_plain(s_rows, S)
+
+        for s in range(SETS):
+            interleave("kn", s, kn_raw[:, s, :].rearrange("p (j n) -> p j n", j=PACK))
+        for s in range(SETS):
+            quantise("kn", s)
+        for s in range(SETS):
+            interleave("u", s, u_moved[s][:])
+            quantise("u", s)
+            product(s, w, "kn", "u")
+        for g in range(HEADS):
+            add_and_store(g)

from contextlib import ExitStack

import concourse.mybir as mybir

F32 = mybir.dt.float32
BF16 = mybir.dt.bfloat16
U32 = mybir.dt.uint32
U8 = mybir.dt.uint8
FP8X4 = mybir.dt.float8_e4m3fn_x4
ALU = mybir.AluOpType
ACT = mybir.ActivationFunctionType

HEADS = 8
W = 128
P = 128
ROWS = 32
PACK = 4
SIDE = P // ROWS
SETS = HEADS // SIDE
PAIR = 2
RUN = 4
LAG = 3

FLOPS = 2 * 2 * HEADS * W * W * W


def tile_rows_upd_huber_kernel(tc, kT, S, v, be, kn, out):
    nc = tc.nc

    with ExitStack() as ctx:
        sb = ctx.enter_context(tc.tile_pool(name="sb", bufs=1))
        ps = ctx.enter_context(tc.psum_pool(name="ps", bufs=1))
        ctx.enter_context(tc.manual_schedule())

        def tiles(name, shape, dtype, count):
            return [sb.tile(shape, dtype, name="%s%d" % (name, n), align_bytes=64) for n in range(count)]

        operands = ("S", "kT", "kn", "u")
        s_raw = tiles("S_raw", [P, PACK, W], F32, SETS)
        kt_raw = tiles("kT_raw", [P, PACK, W], F32, SETS)
        kn_raw = sb.tile([P, SETS, PACK * W], F32, name="kn_raw")
        u_moved = tiles("u_moved", [P, PACK, W], BF16, SETS)
        grouped = {name: tiles(name + "_grouped", [P, W, PACK], BF16, SETS) for name in operands}
        codes = {name: tiles(name + "_codes", [P, W], U32, SETS) for name in operands}
        scales = {name: tiles(name + "_scales", [P, W], U8, SETS) for name in operands}
        v_rows = tiles("v_rows", [P, PAIR, W], F32, HEADS // PAIR)
        s_rows = tiles("s_rows", [P, PAIR, W], F32, HEADS // PAIR)
        err = tiles("err", [P, W], F32, HEADS)
        squashed = tiles("squashed", [P, W], F32, HEADS)
        u_rows = tiles("u_rows", [P, W], BF16, HEADS)
        res = tiles("res", [P, W], F32, HEADS)
        be_raw = sb.tile([P, HEADS * ROWS], F32, name="be_raw", align_bytes=64)
        be_col = sb.tile([P, HEADS * ROWS], F32, name="be_col", align_bytes=64)
        banks = [ps.tile([P, 2, W], F32, name="bank%d" % g) for g in range(HEADS)]
        z = [bank[:, 0, :] for bank in banks]
        w = [bank[:, 1, :] for bank in banks]

        def load_packed(dst, x, s):
            rows = x[SIDE * s : SIDE * (s + 1)].rearrange("c (p j) n -> (c p) j n", j=PACK)
            nc.sync.dma_start(out=dst[s][:], in_=rows)

        def load_plain(dst, x):
            for n in range(HEADS // PAIR):
                nc.sync.dma_start(out=dst[n][:], in_=x[PAIR * n : PAIR * (n + 1)].rearrange("c r n -> r c n"))

        def interleave(name, s, rows):
            nc.vector.tensor_copy(
                out=grouped[name][s][:].rearrange("p (a i) j -> p a j i", i=RUN),
                in_=rows.rearrange("p j (a i) -> p a j i", i=RUN),
            )

        def quantise(name, s):
            nc.vector.quantize_mx(
                out=codes[name][s][:].bitcast(FP8X4),
                scales=scales[name][s][:],
                in_=grouped[name][s][:].rearrange("p n j -> p (n j)"),
            )

        def product(s, results, stationary, moving):
            for c in range(SIDE):
                rows = slice(ROWS * c, ROWS * (c + 1))
                nc.tensor.matmul_mx(
                    out=results[SIDE * s + c],
                    lhsT=codes[stationary][s][rows, :].bitcast(FP8X4),
                    lhsT_scale=scales[stationary][s][rows, :],
                    rhs=codes[moving][s][rows, :].bitcast(FP8X4),
                    rhs_scale=scales[moving][s][rows, :],
                    start=True,
                    stop=True,
                )

        def squash_error(g):
            nc.vector.tensor_tensor(out=err[g][:], in0=v_rows[g // PAIR][:, g % PAIR, :], in1=z[g], op=ALU.subtract)
            nc.scalar.activation(out=squashed[g][:], in_=err[g][:], func=ACT.Tanh)

        def scale_and_move(g):
            s, c = divmod(g, SIDE)
            step = be_col[:, ROWS * g : ROWS * g + 1]
            nc.vector.tensor_scalar(out=u_rows[g][:], in0=squashed[g][:], scalar1=step, scalar2=None, op0=ALU.mult)
            nc.sync.dma_start(out=u_moved[s][ROWS * c : ROWS * (c + 1), :, :], in_=u_rows[g][:])

        def add_and_store(g):
            nc.vector.tensor_tensor(out=res[g][:], in0=s_rows[g // PAIR][:, g % PAIR, :], in1=w[g], op=ALU.add)
            nc.sync.dma_start(out=out[g], in_=res[g][:])

        nc.gpsimd.memset(be_raw[:], 0.0)
        load_packed(s_raw, S, 0)
        load_packed(kt_raw, kT, 0)
        nc.sync.dma_start(
            out=be_raw[0:P:ROWS, :].rearrange("q (g a) -> q g a", a=ROWS),
            in_=be.rearrange("g (q a) o -> q g (a o)", a=ROWS),
        )
        load_packed(s_raw, S, 1)
        load_packed(kt_raw, kT, 1)
        load_plain(v_rows, v)
        nc.sync.dma_start(out=kn_raw[:], in_=kn.rearrange("(s c) (p j) n -> (c p) s (j n)", c=SIDE, j=PACK))

        interleave("S", 0, s_raw[0][:])
        quantise("S", 0)
        interleave("kT", 0, kt_raw[0][:])
        nc.vector.transpose(out=be_col[:], in_=be_raw[:])
        quantise("kT", 0)
        product(0, z, "kT", "S")
        interleave("S", 1, s_raw[1][:])
        interleave("kT", 1, kt_raw[1][:])
        quantise("S", 1)
        quantise("kT", 1)
        product(1, z, "kT", "S")

        for g in range(HEADS + LAG):
            if g < HEADS:
                squash_error(g)
            if g >= LAG:
                scale_and_move(g - LAG)

        load_plain(s_rows, S)

        for s in range(SETS):
            interleave("kn", s, kn_raw[:, s, :].rearrange("p (j n) -> p j n", j=PACK))
        for s in range(SETS):
            quantise("kn", s)
        for s in range(SETS):
            interleave("u", s, u_moved[s][:])
            quantise("u", s)
            product(s, w, "kn", "u")
        for g in range(HEADS):
            add_and_store(g)
